import numpy as np
import ml_dtypes


def mxq(x, axis, fmt="e4m3"):
    dtype, down = {"e4m3": (ml_dtypes.float8_e4m3fn, 7), "e5m2": (ml_dtypes.float8_e5m2, 14)}[fmt]
    v = np.moveaxis(np.asarray(x, np.float32).astype(ml_dtypes.bfloat16).astype(np.float64), axis, -1)
    blocks = v.reshape(v.shape[:-1] + (-1, 32))
    amax = np.abs(blocks).max(-1, keepdims=True)
    byte = np.maximum(np.where(amax > 0, np.frexp(amax)[1] - 1 + 127, 0) - down, 1)
    scale = np.exp2(byte - 127.0)
    codes = (blocks / scale).astype(np.float32).astype(dtype).astype(np.float64)
    return np.moveaxis((codes * scale).reshape(v.shape), -1, axis)


WIDE = False


def mx_kscale(k):
    if not WIDE:
        return np.ones(k)
    levels = np.array([10, -10, 5, -5, 0])
    if k % 512:
        return np.exp2(np.random.permutation(np.resize(levels, k // 32))).repeat(32)
    a = np.empty((k // 512, 16))
    for p in range(k // 512):
        a[p, :8] = np.random.permutation(np.resize(levels, 8))
        for g in range(8):
            far = levels[np.abs(levels - a[p, g]) >= 10]
            a[p, g + 8] = far[np.random.randint(len(far))]
    return np.exp2(a.ravel()).repeat(32)


def f64(x):
    return np.asarray(x).astype(np.float64)


def striped(idx):
    return np.tile(idx.reshape(-1, 16).T, (8, 1)).astype(np.uint16)


def unstriped(offs):
    return offs[:16].T.reshape(-1).astype(np.int64)


def pack_weight(w):
    k, n = w.shape
    w = f64(np.asarray(w, np.float32).astype(ml_dtypes.bfloat16)).reshape(k // 32, 32, n)
    amax = np.abs(w).max(1)
    byte = np.clip(np.where(amax > 0, np.frexp(amax)[1] - 1 + 127 - 7, 1), 1, 254)
    scaled = (w * np.exp2(127.0 - byte)[:, None, :]).reshape(k, n).astype(np.float32)
    words = np.ascontiguousarray(scaled.reshape(k // 512, 128, 4, n).transpose(0, 1, 3, 2)).astype(ml_dtypes.float8_e4m3fn).view(np.uint8)
    return words, np.ascontiguousarray(byte.astype(np.uint8).reshape(k // 512, 16, n))


def unpack_weight(words, scales):
    g, p, n, _ = words.shape
    vals = np.ascontiguousarray(words).view(ml_dtypes.float8_e4m3fn).astype(np.float64) * np.repeat(np.exp2(scales.astype(np.float64) - 127.0), 8, axis=1)[..., None]
    return vals.transpose(0, 1, 3, 2).reshape(g * 512, n)


K, T, S, D, N = 1024, 2048, 1024, 8, 256
P = 2 ** 7


def setup_inputs():
    n = np.random.standard_normal
    s = mx_kscale(K)[:, None]
    packed_xT = pack_weight(n((K, T)) * s)
    return {
        "x_words": packed_xT[0],
        "x_scales": packed_xT[1],
        "w1": (n((K, N)) / np.sqrt(K) / s).astype(np.float32),
        "w2": (n((K, N)) / np.sqrt(K) / s).astype(np.float32),
        "dist": (np.tile(np.random.uniform(0.1, 1.5, S), (P, 1))).astype(np.float32),
        "offs": striped(np.random.permutation(T)[:S]),
    }


def reference(x_words, x_scales, w1, w2, dist, offs):
    xq = unpack_weight(x_words, x_scales)[:, unstriped(offs)]
    ys = mxq(f64(w2), 0, "e4m3").T @ xq
    shp = np.log(np.exp(ys) + 1.0) + 0.3
    sr = shp * f64(dist)[:1]
    prof = shp * ((np.exp(-1.0 * sr) + np.exp(-0.333333 * sr)) / (f64(dist)[:1] + 0.2))
    yi = mxq(f64(w1), 0, "e4m3").T @ xq
    irr = np.exp(0.5 * yi)
    wi = prof * irr
    return (wi.reshape(len(wi), -1, D).sum(axis=2)) / (prof.reshape(len(prof), -1, D).sum(axis=2) + 0.1)

@@ -1,0 +1,261 @@
+import math
+from contextlib import ExitStack
+
+import concourse.mybir as mybir
+from concourse.masks import make_identity
+
+K, T, S, D, N = 1024, 2048, 1024, 8, 256
+FLOPS = 2 * 2 * K * S * N
+
+F32 = mybir.dt.float32
+BF16 = mybir.dt.bfloat16
+I32 = mybir.dt.int32
+U32 = mybir.dt.uint32
+U16 = mybir.dt.uint16
+U8 = mybir.dt.uint8
+FP8X4 = mybir.dt.float8_e4m3fn_x4
+ALU = mybir.AluOpType
+ACT = mybir.ActivationFunctionType
+
+P = 128
+PACK = 4
+PASSES = K // (P * PACK)
+HALVES = 2
+HALF = S // HALVES
+DEAL = HALF // P
+TILES = S // P
+PAIR = D // DEAL
+POINTS = P // PAIR
+M_BLOCKS = N // P
+SHAPE_OFFSET = 0.3
+EXP_CLAMP = 2.0 ** 60
+
+
+def tile_picked_ybssrd_norm_p_kernel(
+    tc, x_words, x_scales, w1, w2, dist, offs, out
+):
+    nc = tc.nc
+    with ExitStack() as ctx:
+        keep = ctx.enter_context(tc.tile_pool(name="keep", bufs=1))
+        psum = ctx.enter_context(tc.psum_pool(name="psum", bufs=1))
+
+        offsets = keep.tile([P, S // 16], U16, name="offsets")
+        nc.sync.dma_start(offsets[:], offs)
+
+        x_plane = keep.tile([P, T], U8, name="x_plane", align_bytes=64)
+        nc.gpsimd.memset(x_plane[:].bitcast(I32), 0)
+        for q in range(4):
+            nc.scalar.dma_start(
+                x_plane[32 * q : 32 * q + 4 * PASSES, :].bitcast(I32),
+                x_scales[:, 4 * q : 4 * q + 4, :].bitcast(I32),
+            )
+
+        def load_words(o):
+            table = keep.tile([P, T], U32, name="x_table%d" % o, align_bytes=64)
+            nc.sync.dma_start(
+                table[:].bitcast(I32), x_words[o].rearrange("p n t -> p (n t)").bitcast(I32)
+            )
+            return table
+
+        def load_weight(w, o, name):
+            raw = keep.tile([P, PACK, N], F32, name="%s_raw%d" % (name, o), tag="raw", bufs=2, align_bytes=64)
+            rows = w[o * P * PACK : (o + 1) * P * PACK, :]
+            nc.sync.dma_start(raw[:], rows.rearrange("(p j) n -> p j n", j=PACK))
+            return raw
+
+        table0 = load_words(0)
+        w2_raw0 = load_weight(w2, 0, "w2")
+        w2_raw1 = load_weight(w2, 1, "w2")
+        table1 = load_words(1)
+        d_col = keep.tile([P, HALVES, DEAL], F32, name="d_col")
+        nc.gpsimd.dma_start(d_col[:], dist[0].rearrange("(h p t) -> p h t", h=HALVES, t=DEAL))
+
+        ident = keep.tile([P, P], F32, name="ident")
+        make_identity(nc, ident[:])
+
+        def interleave(copy, raw, name):
+            grouped = keep.tile([P, N, PACK], BF16, name=name + "_bf16", align_bytes=64)
+            copy(
+                grouped[:].rearrange("p (c i) j -> p c j i", i=4),
+                raw[:].rearrange("p j (c i) -> p c j i", i=4),
+            )
+            return grouped
+
+        def quantize(grouped, name):
+            codes = keep.tile([P, N], U32, name=name + "_codes", align_bytes=64)
+            scales = keep.tile([P, N], U8, name=name + "_scales", align_bytes=64)
+            nc.vector.quantize_mx(
+                out=codes[:].bitcast(FP8X4),
+                scales=scales[:],
+                in_=grouped[:].rearrange("p n j -> p (n j)"),
+            )
+            return codes, scales
+
+        def gather_words(table, o, h):
+            picked = keep.tile([P, HALF], U32, name="picked%d_%d" % (o, h), tag="late%d" % h if o else "early%d" % h, align_bytes=64)
+            cols = HALF // 16
+            nc.vector.tensor_copy(
+                picked[:].rearrange("p (t s) -> p s t", t=DEAL),
+                table[:].indirect(offsets[:, h * cols : (h + 1) * cols]),
+            )
+            return picked
+
+        def gather_scales(h):
+            cols = HALF // 16
+            picked = keep.tile([P, HALF], U8, name="picked_plane%d" % h, tag="late%d" % h, align_bytes=64)
+            nc.vector.tensor_copy(picked[:], x_plane[:].indirect(offsets[:, h * cols : (h + 1) * cols]))
+            return picked
+
+        def deal_scales(picked, h):
+            dealt = keep.tile([P, HALF], U8, name="dealt_plane%d" % h, align_bytes=64)
+            nc.vector.tensor_copy(
+                dealt[:].rearrange("p (t s) -> p t s", t=DEAL),
+                picked[:].rearrange("p (s t) -> p t s", t=DEAL),
+            )
+            return dealt
+
+        w2_bf = [interleave(nc.scalar.copy, raw, "w2_%d" % o) for o, raw in enumerate((w2_raw0, w2_raw1))]
+        w1_raw = [load_weight(w1, o, "w1") for o in range(PASSES)]
+
+        banks = [psum.tile([P, 2, N], F32, name="bank%d" % i, tag="bank%d" % i) for i in range(TILES)]
+        ys = [bank[:, 0, :] for bank in banks]
+        yi = [bank[:, 1, :] for bank in banks]
+        words, planes, w2_q = {}, {}, {}
+
+        def product(i, o, wq, dst):
+            h, t = divmod(i, DEAL)
+            nc.tensor.matmul_mx(
+                out=dst,
+                lhsT=words[o, h][:, t * P : (t + 1) * P].bitcast(FP8X4),
+                lhsT_scale=planes[h][4 * o :, t * P : (t + 1) * P],
+                rhs=wq[o][0][:].bitcast(FP8X4),
+                rhs_scale=wq[o][1][:],
+                start=(o == 0),
+                stop=(o == PASSES - 1),
+            )
+
+        for h in range(HALVES):
+            words[0, h] = gather_words(table0, 0, h)
+        for h in range(HALVES):
+            picked = gather_scales(h)
+            w2_q[h] = quantize(w2_bf[h], "w2_%d" % h)
+            planes[h] = deal_scales(picked, h)
+            for i in range(h * DEAL, (h + 1) * DEAL):
+                product(i, 0, w2_q, ys[i])
+
+        e_ys = keep.tile([P, TILES, N], F32, name="e_ys")
+        for h in range(HALVES):
+            words[1, h] = gather_words(table1, 1, h)
+            for i in range(h * DEAL, (h + 1) * DEAL):
+                product(i, 1, w2_q, ys[i])
+                nc.scalar.activation(e_ys[:, i, :], ys[i], ACT.Exp)
+
+        clamped = keep.tile([P, TILES * N], F32, name="clamped")
+        nc.vector.tensor_scalar(
+            clamped[:], e_ys[:].rearrange("p i n -> p (i n)"), EXP_CLAMP, None, ALU.min
+        )
+
+        w1_bf = [interleave(nc.vector.tensor_copy, w1_raw[o], "w1_%d" % o) for o in range(PASSES)]
+        w1_q = [quantize(w1_bf[o], "w1_%d" % o) for o in range(PASSES)]
+        for i in range(TILES):
+            for o in range(PASSES):
+                product(i, o, w1_q, yi[i])
+
+        d_flat = d_col[:].rearrange("p h t -> p (h t)")
+        neg_d = keep.tile([P, TILES], F32, name="neg_d")
+        neg_third_d = keep.tile([P, TILES], F32, name="neg_third_d")
+        d_shifted = keep.tile([P, TILES], F32, name="d_shifted")
+        inv_d = keep.tile([P, TILES], F32, name="inv_d")
+        nc.vector.tensor_scalar(neg_d[:], d_flat, -1.0, None, ALU.mult)
+        nc.vector.tensor_scalar(neg_third_d[:], d_flat, -0.333333, None, ALU.mult)
+        nc.vector.tensor_scalar(d_shifted[:], d_flat, 0.2, None, ALU.add)
+        nc.vector.reciprocal(inv_d[:], d_shifted[:])
+
+        c = math.exp(SHAPE_OFFSET)
+        logs = {}
+        for g in range(TILES // 2):
+            lg = keep.tile([P, 2 * N], F32, name="log%d" % g)
+            nc.scalar.activation(lg[:], clamped[:, g * 2 * N : (g + 1) * 2 * N], ACT.Ln, bias=c, scale=c)
+            logs[g] = lg
+        shp = [keep.tile([P, 2, N], F32, name="shp%d" % g) for g in range(TILES // 2)]
+        for i in range(TILES):
+            nc.vector.scalar_tensor_tensor(
+                shp[i // 2][:, i % 2, :], ys[i], SHAPE_OFFSET,
+                logs[i // 2][:, (i % 2) * N : (i % 2 + 1) * N], ALU.add, ALU.max,
+            )
+
+        near, far, irr = [], [], []
+        for g in range(TILES // 2):
+            near.append(keep.tile([P, 2, N], F32, name="near%d" % g))
+            far.append(keep.tile([P, 2, N], F32, name="far%d" % g))
+            irr.append(keep.tile([P, 2, N], F32, name="irr%d" % g))
+            for u in range(2):
+                i = 2 * g + u
+                nc.scalar.activation(near[g][:, u, :], shp[g][:, u, :], ACT.Exp, scale=neg_d[:, i : i + 1])
+                nc.scalar.activation(far[g][:, u, :], shp[g][:, u, :], ACT.Exp, scale=neg_third_d[:, i : i + 1])
+            for u in range(2):
+                nc.scalar.activation(irr[g][:, u, :], yi[2 * g + u], ACT.Exp, scale=0.5)
+
+        acc_p = [psum.tile([P, HALVES, P], F32, name="accp%d" % m, tag="bank%d" % m) for m in range(M_BLOCKS)]
+        acc_w = [
+            [psum.tile([P, P], F32, name="accw%d_%d" % (h, m), tag="bank%d" % (2 + 2 * h + m)) for m in range(M_BLOCKS)]
+            for h in range(HALVES)
+        ]
+
+        def add_up(acc, src, i):
+            for m in range(M_BLOCKS):
+                nc.tensor.matmul(
+                    acc[m], src[:, m * P : (m + 1) * P], ident[:], is_transpose=True,
+                    start=(i % DEAL == 0), stop=(i % DEAL == DEAL - 1),
+                )
+
+        den = keep.tile([P, M_BLOCKS, HALVES * POINTS], F32, name="den")
+        num = keep.tile([P, M_BLOCKS, HALVES * POINTS], F32, name="num")
+
+        def sum_pairs_w(h):
+            for m in range(M_BLOCKS):
+                nc.vector.tensor_reduce(
+                    num[:, m, h * POINTS : (h + 1) * POINTS], acc_w[h][m][:].rearrange("p (v e) -> p v e", e=PAIR),
+                    mybir.AxisListType.X, ALU.add,
+                )
+
+        prof = [keep.tile([P, 2, N], F32, name="prof%d" % g) for g in range(TILES // 2)]
+
+        def light(g, parts):
+            h = 2 * g // DEAL
+            lit = keep.tile([P, 2, N], F32, name="lit%d" % g)
+            for part in parts:
+                nc.vector.tensor_tensor(lit[:, part, :], prof[g][:, part, :], irr[g][:, part, :], ALU.mult)
+                for u in range(part.start, part.stop):
+                    add_up([acc[:] for acc in acc_w[h]], lit[:, u, :], 2 * g + u)
+
+        last = TILES // 2 - 1
+        for g in range(TILES // 2):
+            both = keep.tile([P, 2, N], F32, name="both%d" % g)
+            nc.vector.tensor_tensor(both[:], near[g][:], far[g][:], ALU.add)
+            if g > 0:
+                light(g - 1, [slice(0, 2)])
+            if g == last:
+                sum_pairs_w(0)
+            for u in range(2):
+                i = 2 * g + u
+                nc.vector.scalar_tensor_tensor(
+                    prof[g][:, u, :], both[:, u, :], inv_d[:, i : i + 1], shp[g][:, u, :], ALU.mult, ALU.mult
+                )
+                add_up([acc[:, i // DEAL, :] for acc in acc_p], prof[g][:, u, :], i)
+        light(last, [slice(0, 1), slice(1, 2)])
+
+        for m in range(M_BLOCKS):
+            nc.vector.tensor_reduce(
+                den[:, m, :], acc_p[m][:].rearrange("p h (v e) -> p (h v) e", e=PAIR), mybir.AxisListType.X, ALU.add
+            )
+        sum_pairs_w(1)
+        root = keep.tile([P, M_BLOCKS, HALVES * POINTS], F32, name="root")
+        inv = keep.tile([P, M_BLOCKS, HALVES * POINTS], F32, name="inv")
+        res = keep.tile([P, M_BLOCKS, HALVES * POINTS], F32, name="res")
+        for m in range(M_BLOCKS):
+            nc.scalar.activation(root[:, m, :], den[:, m, :], ACT.Abs_reciprocal_sqrt, bias=0.1)
+        for m in range(M_BLOCKS):
+            nc.scalar.activation(inv[:, m, :], root[:, m, :], ACT.Square)
+        nc.vector.tensor_tensor(res[:], num[:], inv[:], ALU.mult)
+        nc.sync.dma_start(out.rearrange("(m p) v -> p m v", p=P), res[:])

@@ -42,7 +42,7 @@ def tile_picked_ybssrd_norm_p_kernel(
         offsets = keep.tile([P, S // 16], U16, name="offsets")
         nc.sync.dma_start(offsets[:], offs)
 
-        x_plane = keep.tile([P, T], U8, name="x_plane", align_bytes=64)
+        x_plane = keep.tile([P, T], U8, name="x_plane", tag="x_plane", align_bytes=64)
         nc.gpsimd.memset(x_plane[:].bitcast(I32), 0)
         for q in range(4):
             nc.scalar.dma_start(
@@ -67,23 +67,21 @@ def tile_picked_ybssrd_norm_p_kernel(
         w2_raw0 = load_weight(w2, 0, "w2")
         w2_raw1 = load_weight(w2, 1, "w2")
         table1 = load_words(1)
-        d_col = keep.tile([P, HALVES, DEAL], F32, name="d_col")
-        nc.gpsimd.dma_start(d_col[:], dist[0].rearrange("(h p t) -> p h t", h=HALVES, t=DEAL))
 
         ident = keep.tile([P, P], F32, name="ident")
         make_identity(nc, ident[:])
 
         def interleave(copy, raw, name):
-            grouped = keep.tile([P, N, PACK], BF16, name=name + "_bf16", align_bytes=64)
+            grouped = keep.tile([P, N, PACK], BF16, name=name + "_bf16", tag=name + "_bf16", align_bytes=64)
             copy(
                 grouped[:].rearrange("p (c i) j -> p c j i", i=4),
                 raw[:].rearrange("p j (c i) -> p c j i", i=4),
             )
             return grouped
 
-        def quantize(grouped, name):
+        def quantize(grouped, name, scales_tag):
             codes = keep.tile([P, N], U32, name=name + "_codes", align_bytes=64)
-            scales = keep.tile([P, N], U8, name=name + "_scales", align_bytes=64)
+            scales = keep.tile([P, N], U8, name=name + "_scales", tag=scales_tag, align_bytes=64)
             nc.vector.quantize_mx(
                 out=codes[:].bitcast(FP8X4),
                 scales=scales[:],
@@ -92,7 +90,7 @@ def tile_picked_ybssrd_norm_p_kernel(
             return codes, scales
 
         def gather_words(table, o, h):
-            picked = keep.tile([P, HALF], U32, name="picked%d_%d" % (o, h), tag="late%d" % h if o else "early%d" % h, align_bytes=64)
+            picked = keep.tile([P, HALF], U32, name="picked%d_%d" % (o, h), tag=("x_plane", "w2_0_bf16")[h] if o else "early%d" % h, align_bytes=64)
             cols = HALF // 16
             nc.vector.tensor_copy(
                 picked[:].rearrange("p (t s) -> p s t", t=DEAL),
@@ -136,12 +134,13 @@ def tile_picked_ybssrd_norm_p_kernel(
 
         for h in range(HALVES):
             words[0, h] = gather_words(table0, 0, h)
+        picked_scales = [gather_scales(h) for h in range(HALVES)]
         for h in range(HALVES):
-            picked = gather_scales(h)
-            w2_q[h] = quantize(w2_bf[h], "w2_%d" % h)
-            planes[h] = deal_scales(picked, h)
-            for i in range(h * DEAL, (h + 1) * DEAL):
-                product(i, 0, w2_q, ys[i])
+            planes[h] = deal_scales(picked_scales[h], h)
+        for o in range(PASSES):
+            w2_q[o] = quantize(w2_bf[o], "w2_%d" % o, "late%d" % o)
+        for i in range(TILES):
+            product(i, 0, w2_q, ys[i])
 
         e_ys = keep.tile([P, TILES, N], F32, name="e_ys")
         for h in range(HALVES):
@@ -156,19 +155,21 @@ def tile_picked_ybssrd_norm_p_kernel(
         )
 
         w1_bf = [interleave(nc.vector.tensor_copy, w1_raw[o], "w1_%d" % o) for o in range(PASSES)]
-        w1_q = [quantize(w1_bf[o], "w1_%d" % o) for o in range(PASSES)]
+        w1_q = [quantize(w1_bf[o], "w1_%d" % o, "w1_scales%d" % o) for o in range(PASSES)]
         for i in range(TILES):
             for o in range(PASSES):
                 product(i, o, w1_q, yi[i])
 
+        d_col = keep.tile([P, HALVES, DEAL], F32, name="d_col", tag="w2_1_bf16", align_bytes=64)
+        nc.sync.dma_start(d_col[:], dist[0].rearrange("(h p t) -> p h t", h=HALVES, t=DEAL))
         d_flat = d_col[:].rearrange("p h t -> p (h t)")
         neg_d = keep.tile([P, TILES], F32, name="neg_d")
         neg_third_d = keep.tile([P, TILES], F32, name="neg_third_d")
         d_shifted = keep.tile([P, TILES], F32, name="d_shifted")
         inv_d = keep.tile([P, TILES], F32, name="inv_d")
-        nc.vector.tensor_scalar(neg_d[:], d_flat, -1.0, None, ALU.mult)
-        nc.vector.tensor_scalar(neg_third_d[:], d_flat, -0.333333, None, ALU.mult)
-        nc.vector.tensor_scalar(d_shifted[:], d_flat, 0.2, None, ALU.add)
+        nc.gpsimd.tensor_scalar(neg_d[:], d_flat, -1.0, None, ALU.mult)
+        nc.gpsimd.tensor_scalar(neg_third_d[:], d_flat, -0.333333, None, ALU.mult)
+        nc.gpsimd.tensor_scalar(d_shifted[:], d_flat, 0.2, None, ALU.add)
         nc.vector.reciprocal(inv_d[:], d_shifted[:])
 
         c = math.exp(SHAPE_OFFSET)
@@ -186,7 +187,7 @@ def tile_picked_ybssrd_norm_p_kernel(
 
         near, far, irr = [], [], []
         for g in range(TILES // 2):
-            near.append(keep.tile([P, 2, N], F32, name="near%d" % g))
+            near.append(keep.tile([P, 2, N], F32, name="near%d" % g, tag="near%d" % g))
             far.append(keep.tile([P, 2, N], F32, name="far%d" % g))
             irr.append(keep.tile([P, 2, N], F32, name="irr%d" % g))
             for u in range(2):
@@ -196,66 +197,79 @@ def tile_picked_ybssrd_norm_p_kernel(
             for u in range(2):
                 nc.scalar.activation(irr[g][:, u, :], yi[2 * g + u], ACT.Exp, scale=0.5)
 
-        acc_p = [psum.tile([P, HALVES, P], F32, name="accp%d" % m, tag="bank%d" % m) for m in range(M_BLOCKS)]
-        acc_w = [
-            [psum.tile([P, P], F32, name="accw%d_%d" % (h, m), tag="bank%d" % (2 + 2 * h + m)) for m in range(M_BLOCKS)]
-            for h in range(HALVES)
-        ]
+        def open_sums(name, first_bank):
+            return psum.tile([P, M_BLOCKS, P], F32, name=name, tag="bank%d" % first_bank)
 
         def add_up(acc, src, i):
             for m in range(M_BLOCKS):
                 nc.tensor.matmul(
-                    acc[m], src[:, m * P : (m + 1) * P], ident[:], is_transpose=True,
-                    start=(i % DEAL == 0), stop=(i % DEAL == DEAL - 1),
+                    acc[:, m, :], src[:, m * P : (m + 1) * P], ident[:], is_transpose=True,
+                    start=(i % DEAL == 0 and m == 0), stop=(i % DEAL == DEAL - 1 and m == M_BLOCKS - 1),
                 )
 
-        den = keep.tile([P, M_BLOCKS, HALVES * POINTS], F32, name="den")
-        num = keep.tile([P, M_BLOCKS, HALVES * POINTS], F32, name="num")
+        def sum_pairs(dst, acc):
+            nc.vector.tensor_reduce(
+                dst[:].rearrange("p m v -> p (m v)"), acc[:].rearrange("p m (v e) -> p (m v) e", e=PAIR),
+                mybir.AxisListType.X, ALU.add,
+            )
 
-        def sum_pairs_w(h):
-            for m in range(M_BLOCKS):
-                nc.vector.tensor_reduce(
-                    num[:, m, h * POINTS : (h + 1) * POINTS], acc_w[h][m][:].rearrange("p (v e) -> p v e", e=PAIR),
-                    mybir.AxisListType.X, ALU.add,
-                )
-
+        den = [keep.tile([P, M_BLOCKS, POINTS], F32, name="den%d" % h) for h in range(HALVES)]
+        num = [keep.tile([P, M_BLOCKS, POINTS], F32, name="num%d" % h) for h in range(HALVES)]
         prof = [keep.tile([P, 2, N], F32, name="prof%d" % g) for g in range(TILES // 2)]
+        acc_p, acc_w, lits = {}, {}, {}
 
-        def light(g, parts):
-            h = 2 * g // DEAL
-            lit = keep.tile([P, 2, N], F32, name="lit%d" % g)
-            for part in parts:
-                nc.vector.tensor_tensor(lit[:, part, :], prof[g][:, part, :], irr[g][:, part, :], ALU.mult)
-                for u in range(part.start, part.stop):
-                    add_up([acc[:] for acc in acc_w[h]], lit[:, u, :], 2 * g + u)
-
-        last = TILES // 2 - 1
-        for g in range(TILES // 2):
+        def add_exponentials(g, parts):
             both = keep.tile([P, 2, N], F32, name="both%d" % g)
-            nc.vector.tensor_tensor(both[:], near[g][:], far[g][:], ALU.add)
-            if g > 0:
-                light(g - 1, [slice(0, 2)])
-            if g == last:
-                sum_pairs_w(0)
+            for part in parts:
+                nc.vector.tensor_tensor(both[:, part, :], near[g][:, part, :], far[g][:, part, :], ALU.add)
+            return both
+
+        def profile(g, both):
+            h = 2 * g // DEAL
+            if h not in acc_p:
+                acc_p[h] = open_sums("accp%d" % h, 2 * h)
             for u in range(2):
                 i = 2 * g + u
                 nc.vector.scalar_tensor_tensor(
                     prof[g][:, u, :], both[:, u, :], inv_d[:, i : i + 1], shp[g][:, u, :], ALU.mult, ALU.mult
                 )
-                add_up([acc[:, i // DEAL, :] for acc in acc_p], prof[g][:, u, :], i)
-        light(last, [slice(0, 1), slice(1, 2)])
+                add_up(acc_p[h], prof[g][:, u, :], i)
 
-        for m in range(M_BLOCKS):
-            nc.vector.tensor_reduce(
-                den[:, m, :], acc_p[m][:].rearrange("p h (v e) -> p (h v) e", e=PAIR), mybir.AxisListType.X, ALU.add
-            )
-        sum_pairs_w(1)
-        root = keep.tile([P, M_BLOCKS, HALVES * POINTS], F32, name="root")
-        inv = keep.tile([P, M_BLOCKS, HALVES * POINTS], F32, name="inv")
-        res = keep.tile([P, M_BLOCKS, HALVES * POINTS], F32, name="res")
-        for m in range(M_BLOCKS):
-            nc.scalar.activation(root[:, m, :], den[:, m, :], ACT.Abs_reciprocal_sqrt, bias=0.1)
-        for m in range(M_BLOCKS):
-            nc.scalar.activation(inv[:, m, :], root[:, m, :], ACT.Square)
-        nc.vector.tensor_tensor(res[:], num[:], inv[:], ALU.mult)
-        nc.sync.dma_start(out.rearrange("(m p) v -> p m v", p=P), res[:])
+        def light(g, parts):
+            h = 2 * g // DEAL
+            if h not in acc_w:
+                acc_w[h] = open_sums("accw%d" % h, 2 * h + 1)
+            if g not in lits:
+                lits[g] = keep.tile([P, 2, N], F32, name="lit%d" % g)
+            lit = lits[g]
+            for part in parts:
+                nc.vector.tensor_tensor(lit[:, part, :], prof[g][:, part, :], irr[g][:, part, :], ALU.mult)
+                for u in range(part.start, part.stop):
+                    add_up(acc_w[h], lit[:, u, :], 2 * g + u)
+
+        whole = [slice(0, 2)]
+        profile(0, add_exponentials(0, [slice(0, 1), slice(1, 2)]))
+        both = add_exponentials(1, whole)
+        light(0, whole)
+        profile(1, both)
+        both = add_exponentials(2, whole)
+        light(1, whole)
+        sum_pairs(den[0], acc_p[0])
+        profile(2, both)
+        both = add_exponentials(3, whole)
+        light(2, whole)
+        profile(3, both)
+        sum_pairs(num[0], acc_w[0])
+        light(3, [slice(0, 1)])
+        sum_pairs(den[1], acc_p[1])
+        light(3, [slice(1, 2)])
+        sum_pairs(num[1], acc_w[1])
+
+        res = keep.tile([P, M_BLOCKS, HALVES, POINTS], F32, name="res")
+        for h in range(HALVES):
+            root = keep.tile([P, M_BLOCKS, POINTS], F32, name="root%d" % h, tag="near%d" % (3 - h))
+            inv = keep.tile([P, M_BLOCKS, POINTS], F32, name="inv%d" % h)
+            nc.scalar.activation(root[:], den[h][:], ACT.Abs_reciprocal_sqrt, bias=0.1)
+            nc.scalar.activation(inv[:], root[:], ACT.Square)
+            nc.vector.tensor_tensor(res[:, :, h, :], num[h][:], inv[:], ALU.mult)
+        nc.sync.dma_start(out.rearrange("(m p) v -> p m v", p=P), res[:].rearrange("p m h v -> p m (h v)"))

@@ -29,6 +29,7 @@ POINTS = P // PAIR
 M_BLOCKS = N // P
 SHAPE_OFFSET = 0.3
 EXP_CLAMP = 2.0 ** 60
+WARM_PASSES = 4
 
 
 def tile_picked_ybssrd_norm_p_kernel(
@@ -43,7 +44,7 @@ def tile_picked_ybssrd_norm_p_kernel(
         nc.sync.dma_start(offsets[:], offs)
 
         x_plane = keep.tile([P, T], U8, name="x_plane", tag="x_plane", align_bytes=64)
-        nc.gpsimd.memset(x_plane[:].bitcast(I32), 0)
+        nc.vector.memset(x_plane[:].bitcast(I32), 0)
         for q in range(4):
             nc.scalar.dma_start(
                 x_plane[32 * q : 32 * q + 4 * PASSES, :].bitcast(I32),
@@ -51,7 +52,7 @@ def tile_picked_ybssrd_norm_p_kernel(
             )
 
         def load_words(o):
-            table = keep.tile([P, T], U32, name="x_table%d" % o, align_bytes=64)
+            table = keep.tile([P, T], U32, name="x_table%d" % o, tag="x_table%d" % o, align_bytes=64)
             nc.sync.dma_start(
                 table[:].bitcast(I32), x_words[o].rearrange("p n t -> p (n t)").bitcast(I32)
             )
@@ -90,7 +91,7 @@ def tile_picked_ybssrd_norm_p_kernel(
             return codes, scales
 
         def gather_words(table, o, h):
-            picked = keep.tile([P, HALF], U32, name="picked%d_%d" % (o, h), tag=("x_plane", "w2_0_bf16")[h] if o else "early%d" % h, align_bytes=64)
+            picked = keep.tile([P, HALF], U32, name="picked%d_%d" % (o, h), tag=("x_plane", "w2_1_bf16")[h] if o else "early%d" % h, align_bytes=64)
             cols = HALF // 16
             nc.vector.tensor_copy(
                 picked[:].rearrange("p (t s) -> p s t", t=DEAL),
@@ -115,6 +116,7 @@ def tile_picked_ybssrd_norm_p_kernel(
         w2_bf = [interleave(nc.scalar.copy, raw, "w2_%d" % o) for o, raw in enumerate((w2_raw0, w2_raw1))]
         w1_raw = [load_weight(w1, o, "w1") for o in range(PASSES)]
 
+        warm = psum.tile([P, HALF], F32, name="warm", tag="bank%d" % (TILES - 1))
         banks = [psum.tile([P, 2, N], F32, name="bank%d" % i, tag="bank%d" % i) for i in range(TILES)]
         ys = [bank[:, 0, :] for bank in banks]
         yi = [bank[:, 1, :] for bank in banks]
@@ -134,55 +136,63 @@ def tile_picked_ybssrd_norm_p_kernel(
 
         for h in range(HALVES):
             words[0, h] = gather_words(table0, 0, h)
-        picked_scales = [gather_scales(h) for h in range(HALVES)]
         for h in range(HALVES):
-            planes[h] = deal_scales(picked_scales[h], h)
-        for o in range(PASSES):
-            w2_q[o] = quantize(w2_bf[o], "w2_%d" % o, "late%d" % o)
-        for i in range(TILES):
-            product(i, 0, w2_q, ys[i])
+            picked_scales = gather_scales(h)
+            if h == 0:
+                for u in range(WARM_PASSES):
+                    nc.tensor.matmul_mx(
+                        out=warm[:],
+                        lhsT=words[0, 0][:, :P].bitcast(FP8X4),
+                        lhsT_scale=picked_scales[:, :P],
+                        rhs=words[0, 0][:].bitcast(FP8X4),
+                        rhs_scale=picked_scales[:],
+                        start=True,
+                        stop=True,
+                    )
+            planes[h] = deal_scales(picked_scales, h)
+            w2_q[h] = quantize(w2_bf[h], "w2_%d" % h, "w2_scales%d" % h)
+            for i in range(h * DEAL, (h + 1) * DEAL):
+                product(i, 0, w2_q, ys[i])
 
-        e_ys = keep.tile([P, TILES, N], F32, name="e_ys")
+        clamped = keep.tile([P, HALVES, DEAL, N], F32, name="clamped")
         for h in range(HALVES):
+            e_ys = keep.tile([P, DEAL, N], F32, name="e_ys%d" % h)
             words[1, h] = gather_words(table1, 1, h)
             for i in range(h * DEAL, (h + 1) * DEAL):
                 product(i, 1, w2_q, ys[i])
-                nc.scalar.activation(e_ys[:, i, :], ys[i], ACT.Exp)
+                nc.scalar.activation(e_ys[:, i % DEAL, :], ys[i], ACT.Exp)
+            nc.vector.tensor_scalar(clamped[:, h, :, :], e_ys[:], EXP_CLAMP, None, ALU.min)
 
-        clamped = keep.tile([P, TILES * N], F32, name="clamped")
-        nc.vector.tensor_scalar(
-            clamped[:], e_ys[:].rearrange("p i n -> p (i n)"), EXP_CLAMP, None, ALU.min
-        )
 
         w1_bf = [interleave(nc.vector.tensor_copy, w1_raw[o], "w1_%d" % o) for o in range(PASSES)]
         w1_q = [quantize(w1_bf[o], "w1_%d" % o, "w1_scales%d" % o) for o in range(PASSES)]
-        for i in range(TILES):
+        by_slot = [h * DEAL + t for t in range(DEAL) for h in range(HALVES)]
+        for i in by_slot:
             for o in range(PASSES):
                 product(i, o, w1_q, yi[i])
 
-        d_col = keep.tile([P, HALVES, DEAL], F32, name="d_col", tag="w2_1_bf16", align_bytes=64)
-        nc.sync.dma_start(d_col[:], dist[0].rearrange("(h p t) -> p h t", h=HALVES, t=DEAL))
-        d_flat = d_col[:].rearrange("p h t -> p (h t)")
+        d_col = keep.tile([P, HALVES, 2 * DEAL], F32, name="d_col", tag="x_table0", align_bytes=64)
+        d_flat = d_col[:, :, :DEAL]
+        nc.sync.dma_start(d_flat, dist[0].rearrange("(h p t) -> p h t", h=HALVES, t=DEAL))
         neg_d = keep.tile([P, TILES], F32, name="neg_d")
         neg_third_d = keep.tile([P, TILES], F32, name="neg_third_d")
         d_shifted = keep.tile([P, TILES], F32, name="d_shifted")
-        inv_d = keep.tile([P, TILES], F32, name="inv_d")
-        nc.gpsimd.tensor_scalar(neg_d[:], d_flat, -1.0, None, ALU.mult)
-        nc.gpsimd.tensor_scalar(neg_third_d[:], d_flat, -0.333333, None, ALU.mult)
-        nc.gpsimd.tensor_scalar(d_shifted[:], d_flat, 0.2, None, ALU.add)
+        inv_d = keep.tile([P, TILES], F32, name="inv_d", tag="w1_1_bf16", align_bytes=64)
+        nc.gpsimd.tensor_scalar(neg_d[:].rearrange("p (h t) -> p h t", h=HALVES), d_flat, -1.0, None, ALU.mult)
+        nc.gpsimd.tensor_scalar(neg_third_d[:].rearrange("p (h t) -> p h t", h=HALVES), d_flat, -0.333333, None, ALU.mult)
+        nc.gpsimd.tensor_scalar(d_shifted[:].rearrange("p (h t) -> p h t", h=HALVES), d_flat, 0.2, None, ALU.add)
         nc.vector.reciprocal(inv_d[:], d_shifted[:])
 
         c = math.exp(SHAPE_OFFSET)
-        logs = {}
-        for g in range(TILES // 2):
-            lg = keep.tile([P, 2 * N], F32, name="log%d" % g)
-            nc.scalar.activation(lg[:], clamped[:, g * 2 * N : (g + 1) * 2 * N], ACT.Ln, bias=c, scale=c)
-            logs[g] = lg
+        logs = []
+        for t in range(DEAL):
+            lg = keep.tile([P, HALVES, N], F32, name="log%d" % t)
+            nc.scalar.activation(lg[:], clamped[:, :, t, :], ACT.Ln, bias=c, scale=c)
+            logs.append(lg)
         shp = [keep.tile([P, 2, N], F32, name="shp%d" % g) for g in range(TILES // 2)]
-        for i in range(TILES):
+        for i in by_slot:
             nc.vector.scalar_tensor_tensor(
-                shp[i // 2][:, i % 2, :], ys[i], SHAPE_OFFSET,
-                logs[i // 2][:, (i % 2) * N : (i % 2 + 1) * N], ALU.add, ALU.max,
+                shp[i // 2][:, i % 2, :], ys[i], SHAPE_OFFSET, logs[i % DEAL][:, i // DEAL, :], ALU.add, ALU.max
             )
 
         near, far, irr = [], [], []

@@ -38,6 +38,7 @@ def tile_picked_ybssrd_norm_p_kernel(
     nc = tc.nc
     with ExitStack() as ctx:
         keep = ctx.enter_context(tc.tile_pool(name="keep", bufs=1))
+        stage = ctx.enter_context(tc.tile_pool(name="stage", bufs=1))
         psum = ctx.enter_context(tc.psum_pool(name="psum", bufs=1))
 
         offsets = keep.tile([P, S // 16], U16, name="offsets")
@@ -45,21 +46,25 @@ def tile_picked_ybssrd_norm_p_kernel(
 
         x_plane = keep.tile([P, T], U8, name="x_plane", tag="x_plane", align_bytes=64)
         nc.vector.memset(x_plane[:].bitcast(I32), 0)
+        ones = stage.tile([P, T + 2 * PACK * N], F32, name="ones", offset=4 * T, align_bytes=64)
+        c_col = keep.tile([P, 1], F32, name="c_col")
+        nc.vector.memset(ones[:, :1], 1.0)
+        nc.vector.tensor_scalar(c_col[:], ones[:, :1], math.exp(SHAPE_OFFSET), None, ALU.mult)
         for q in range(4):
-            nc.scalar.dma_start(
+            nc.sync.dma_start(
                 x_plane[32 * q : 32 * q + 4 * PASSES, :].bitcast(I32),
                 x_scales[:, 4 * q : 4 * q + 4, :].bitcast(I32),
             )
 
         def load_words(o):
-            table = keep.tile([P, T], U32, name="x_table%d" % o, tag="x_table%d" % o, align_bytes=64)
+            table = stage.tile([P, T], U32, name="x_table%d" % o, offset=4 * T * o, align_bytes=64)
             nc.sync.dma_start(
                 table[:].bitcast(I32), x_words[o].rearrange("p n t -> p (n t)").bitcast(I32)
             )
             return table
 
         def load_weight(w, o, name):
-            raw = keep.tile([P, PACK, N], F32, name="%s_raw%d" % (name, o), tag="raw", bufs=2, align_bytes=64)
+            raw = stage.tile([P, PACK, N], F32, name="%s_raw%d" % (name, o), offset=4 * (2 * T + o * PACK * N), align_bytes=64)
             rows = w[o * P * PACK : (o + 1) * P * PACK, :]
             nc.sync.dma_start(raw[:], rows.rearrange("(p j) n -> p j n", j=PACK))
             return raw
@@ -171,7 +176,7 @@ def tile_picked_ybssrd_norm_p_kernel(
             for o in range(PASSES):
                 product(i, o, w1_q, yi[i])
 
-        d_col = keep.tile([P, HALVES, 2 * DEAL], F32, name="d_col", tag="x_table0", align_bytes=64)
+        d_col = stage.tile([P, HALVES, 2 * DEAL], F32, name="d_col", offset=0, align_bytes=64)
         d_flat = d_col[:, :, :DEAL]
         nc.sync.dma_start(d_flat, dist[0].rearrange("(h p t) -> p h t", h=HALVES, t=DEAL))
         neg_d = keep.tile([P, TILES], F32, name="neg_d")
@@ -183,11 +188,10 @@ def tile_picked_ybssrd_norm_p_kernel(
         nc.gpsimd.tensor_scalar(d_shifted[:].rearrange("p (h t) -> p h t", h=HALVES), d_flat, 0.2, None, ALU.add)
         nc.vector.reciprocal(inv_d[:], d_shifted[:])
 
-        c = math.exp(SHAPE_OFFSET)
         logs = []
         for t in range(DEAL):
             lg = keep.tile([P, HALVES, N], F32, name="log%d" % t)
-            nc.scalar.activation(lg[:], clamped[:, :, t, :], ACT.Ln, bias=c, scale=c)
+            nc.scalar.activation(lg[:], clamped[:, :, t, :], ACT.Ln, bias=c_col[:], scale=c_col[:])
             logs.append(lg)
         shp = [keep.tile([P, 2, N], F32, name="shp%d" % g) for g in range(TILES // 2)]
         for i in by_slot:

import math
from contextlib import ExitStack

import concourse.mybir as mybir
from concourse.masks import make_identity

K, T, S, D, N = 1024, 2048, 1024, 8, 256
FLOPS = 2 * 2 * K * S * N

F32 = mybir.dt.float32
BF16 = mybir.dt.bfloat16
I32 = mybir.dt.int32
U32 = mybir.dt.uint32
U16 = mybir.dt.uint16
U8 = mybir.dt.uint8
FP8X4 = mybir.dt.float8_e4m3fn_x4
ALU = mybir.AluOpType
ACT = mybir.ActivationFunctionType

P = 128
PACK = 4
PASSES = K // (P * PACK)
HALVES = 2
HALF = S // HALVES
DEAL = HALF // P
TILES = S // P
PAIR = D // DEAL
POINTS = P // PAIR
M_BLOCKS = N // P
SHAPE_OFFSET = 0.3
EXP_CLAMP = 2.0 ** 60
WARM_PASSES = 4


def tile_picked_ybssrd_norm_p_kernel(
    tc, x_words, x_scales, w1, w2, dist, offs, out
):
    nc = tc.nc
    with ExitStack() as ctx:
        keep = ctx.enter_context(tc.tile_pool(name="keep", bufs=1))
        stage = ctx.enter_context(tc.tile_pool(name="stage", bufs=1))
        psum = ctx.enter_context(tc.psum_pool(name="psum", bufs=1))

        offsets = keep.tile([P, S // 16], U16, name="offsets")
        nc.sync.dma_start(offsets[:], offs)

        x_plane = keep.tile([P, T], U8, name="x_plane", tag="x_plane", align_bytes=64)
        nc.vector.memset(x_plane[:].bitcast(I32), 0)
        ones = stage.tile([P, T + 2 * PACK * N], F32, name="ones", offset=4 * T, align_bytes=64)
        c_col = keep.tile([P, 1], F32, name="c_col")
        nc.vector.memset(ones[:, :1], 1.0)
        nc.vector.tensor_scalar(c_col[:], ones[:, :1], math.exp(SHAPE_OFFSET), None, ALU.mult)
        for q in range(4):
            nc.sync.dma_start(
                x_plane[32 * q : 32 * q + 4 * PASSES, :].bitcast(I32),
                x_scales[:, 4 * q : 4 * q + 4, :].bitcast(I32),
            )

        def load_words(o):
            table = stage.tile([P, T], U32, name="x_table%d" % o, offset=4 * T * o, align_bytes=64)
            nc.sync.dma_start(
                table[:].bitcast(I32), x_words[o].rearrange("p n t -> p (n t)").bitcast(I32)
            )
            return table

        def load_weight(w, o, name):
            raw = stage.tile([P, PACK, N], F32, name="%s_raw%d" % (name, o), offset=4 * (2 * T + o * PACK * N), align_bytes=64)
            rows = w[o * P * PACK : (o + 1) * P * PACK, :]
            nc.sync.dma_start(raw[:], rows.rearrange("(p j) n -> p j n", j=PACK))
            return raw

        table0 = load_words(0)
        w2_raw0 = load_weight(w2, 0, "w2")
        w2_raw1 = load_weight(w2, 1, "w2")
        table1 = load_words(1)

        ident = keep.tile([P, P], F32, name="ident")
        make_identity(nc, ident[:])

        def interleave(copy, raw, name):
            grouped = keep.tile([P, N, PACK], BF16, name=name + "_bf16", tag=name + "_bf16", align_bytes=64)
            copy(
                grouped[:].rearrange("p (c i) j -> p c j i", i=4),
                raw[:].rearrange("p j (c i) -> p c j i", i=4),
            )
            return grouped

        def quantize(grouped, name, scales_tag):
            codes = keep.tile([P, N], U32, name=name + "_codes", align_bytes=64)
            scales = keep.tile([P, N], U8, name=name + "_scales", tag=scales_tag, align_bytes=64)
            nc.vector.quantize_mx(
                out=codes[:].bitcast(FP8X4),
                scales=scales[:],
                in_=grouped[:].rearrange("p n j -> p (n j)"),
            )
            return codes, scales

        def gather_words(table, o, h):
            picked = keep.tile([P, HALF], U32, name="picked%d_%d" % (o, h), tag=("x_plane", "w2_1_bf16")[h] if o else "early%d" % h, align_bytes=64)
            cols = HALF // 16
            nc.vector.tensor_copy(
                picked[:].rearrange("p (t s) -> p s t", t=DEAL),
                table[:].indirect(offsets[:, h * cols : (h + 1) * cols]),
            )
            return picked

        def gather_scales(h):
            cols = HALF // 16
            picked = keep.tile([P, HALF], U8, name="picked_plane%d" % h, tag="late%d" % h, align_bytes=64)
            nc.vector.tensor_copy(picked[:], x_plane[:].indirect(offsets[:, h * cols : (h + 1) * cols]))
            return picked

        def deal_scales(picked, h):
            dealt = keep.tile([P, HALF], U8, name="dealt_plane%d" % h, align_bytes=64)
            nc.vector.tensor_copy(
                dealt[:].rearrange("p (t s) -> p t s", t=DEAL),
                picked[:].rearrange("p (s t) -> p t s", t=DEAL),
            )
            return dealt

        w2_bf = [interleave(nc.scalar.copy, raw, "w2_%d" % o) for o, raw in enumerate((w2_raw0, w2_raw1))]
        w1_raw = [load_weight(w1, o, "w1") for o in range(PASSES)]

        warm = psum.tile([P, HALF], F32, name="warm", tag="bank%d" % (TILES - 1))
        banks = [psum.tile([P, 2, N], F32, name="bank%d" % i, tag="bank%d" % i) for i in range(TILES)]
        ys = [bank[:, 0, :] for bank in banks]
        yi = [bank[:, 1, :] for bank in banks]
        words, planes, w2_q = {}, {}, {}

        def product(i, o, wq, dst):
            h, t = divmod(i, DEAL)
            nc.tensor.matmul_mx(
                out=dst,
                lhsT=words[o, h][:, t * P : (t + 1) * P].bitcast(FP8X4),
                lhsT_scale=planes[h][4 * o :, t * P : (t + 1) * P],
                rhs=wq[o][0][:].bitcast(FP8X4),
                rhs_scale=wq[o][1][:],
                start=(o == 0),
                stop=(o == PASSES - 1),
            )

        for h in range(HALVES):
            words[0, h] = gather_words(table0, 0, h)
        for h in range(HALVES):
            picked_scales = gather_scales(h)
            if h == 0:
                for u in range(WARM_PASSES):
                    nc.tensor.matmul_mx(
                        out=warm[:],
                        lhsT=words[0, 0][:, :P].bitcast(FP8X4),
                        lhsT_scale=picked_scales[:, :P],
                        rhs=words[0, 0][:].bitcast(FP8X4),
                        rhs_scale=picked_scales[:],
                        start=True,
                        stop=True,
                    )
            planes[h] = deal_scales(picked_scales, h)
            w2_q[h] = quantize(w2_bf[h], "w2_%d" % h, "w2_scales%d" % h)
            for i in range(h * DEAL, (h + 1) * DEAL):
                product(i, 0, w2_q, ys[i])

        clamped = keep.tile([P, HALVES, DEAL, N], F32, name="clamped")
        for h in range(HALVES):
            e_ys = keep.tile([P, DEAL, N], F32, name="e_ys%d" % h)
            words[1, h] = gather_words(table1, 1, h)
            for i in range(h * DEAL, (h + 1) * DEAL):
                product(i, 1, w2_q, ys[i])
                nc.scalar.activation(e_ys[:, i % DEAL, :], ys[i], ACT.Exp)
            nc.vector.tensor_scalar(clamped[:, h, :, :], e_ys[:], EXP_CLAMP, None, ALU.min)


        w1_bf = [interleave(nc.vector.tensor_copy, w1_raw[o], "w1_%d" % o) for o in range(PASSES)]
        w1_q = [quantize(w1_bf[o], "w1_%d" % o, "w1_scales%d" % o) for o in range(PASSES)]
        by_slot = [h * DEAL + t for t in range(DEAL) for h in range(HALVES)]
        for i in by_slot:
            for o in range(PASSES):
                product(i, o, w1_q, yi[i])

        d_col = stage.tile([P, HALVES, 2 * DEAL], F32, name="d_col", offset=0, align_bytes=64)
        d_flat = d_col[:, :, :DEAL]
        nc.sync.dma_start(d_flat, dist[0].rearrange("(h p t) -> p h t", h=HALVES, t=DEAL))
        neg_d = keep.tile([P, TILES], F32, name="neg_d")
        neg_third_d = keep.tile([P, TILES], F32, name="neg_third_d")
        d_shifted = keep.tile([P, TILES], F32, name="d_shifted")
        inv_d = keep.tile([P, TILES], F32, name="inv_d", tag="w1_1_bf16", align_bytes=64)
        nc.gpsimd.tensor_scalar(neg_d[:].rearrange("p (h t) -> p h t", h=HALVES), d_flat, -1.0, None, ALU.mult)
        nc.gpsimd.tensor_scalar(neg_third_d[:].rearrange("p (h t) -> p h t", h=HALVES), d_flat, -0.333333, None, ALU.mult)
        nc.gpsimd.tensor_scalar(d_shifted[:].rearrange("p (h t) -> p h t", h=HALVES), d_flat, 0.2, None, ALU.add)
        nc.vector.reciprocal(inv_d[:], d_shifted[:])

        logs = []
        for t in range(DEAL):
            lg = keep.tile([P, HALVES, N], F32, name="log%d" % t)
            nc.scalar.activation(lg[:], clamped[:, :, t, :], ACT.Ln, bias=c_col[:], scale=c_col[:])
            logs.append(lg)
        shp = [keep.tile([P, 2, N], F32, name="shp%d" % g) for g in range(TILES // 2)]
        for i in by_slot:
            nc.vector.scalar_tensor_tensor(
                shp[i // 2][:, i % 2, :], ys[i], SHAPE_OFFSET, logs[i % DEAL][:, i // DEAL, :], ALU.add, ALU.max
            )

        near, far, irr = [], [], []
        for g in range(TILES // 2):
            near.append(keep.tile([P, 2, N], F32, name="near%d" % g, tag="near%d" % g))
            far.append(keep.tile([P, 2, N], F32, name="far%d" % g))
            irr.append(keep.tile([P, 2, N], F32, name="irr%d" % g))
            for u in range(2):
                i = 2 * g + u
                nc.scalar.activation(near[g][:, u, :], shp[g][:, u, :], ACT.Exp, scale=neg_d[:, i : i + 1])
                nc.scalar.activation(far[g][:, u, :], shp[g][:, u, :], ACT.Exp, scale=neg_third_d[:, i : i + 1])
            for u in range(2):
                nc.scalar.activation(irr[g][:, u, :], yi[2 * g + u], ACT.Exp, scale=0.5)

        def open_sums(name, first_bank):
            return psum.tile([P, M_BLOCKS, P], F32, name=name, tag="bank%d" % first_bank)

        def add_up(acc, src, i):
            for m in range(M_BLOCKS):
                nc.tensor.matmul(
                    acc[:, m, :], src[:, m * P : (m + 1) * P], ident[:], is_transpose=True,
                    start=(i % DEAL == 0 and m == 0), stop=(i % DEAL == DEAL - 1 and m == M_BLOCKS - 1),
                )

        def sum_pairs(dst, acc):
            nc.vector.tensor_reduce(
                dst[:].rearrange("p m v -> p (m v)"), acc[:].rearrange("p m (v e) -> p (m v) e", e=PAIR),
                mybir.AxisListType.X, ALU.add,
            )

        den = [keep.tile([P, M_BLOCKS, POINTS], F32, name="den%d" % h) for h in range(HALVES)]
        num = [keep.tile([P, M_BLOCKS, POINTS], F32, name="num%d" % h) for h in range(HALVES)]
        prof = [keep.tile([P, 2, N], F32, name="prof%d" % g) for g in range(TILES // 2)]
        acc_p, acc_w, lits = {}, {}, {}

        def add_exponentials(g, parts):
            both = keep.tile([P, 2, N], F32, name="both%d" % g)
            for part in parts:
                nc.vector.tensor_tensor(both[:, part, :], near[g][:, part, :], far[g][:, part, :], ALU.add)
            return both

        def profile(g, both):
            h = 2 * g // DEAL
            if h not in acc_p:
                acc_p[h] = open_sums("accp%d" % h, 2 * h)
            for u in range(2):
                i = 2 * g + u
                nc.vector.scalar_tensor_tensor(
                    prof[g][:, u, :], both[:, u, :], inv_d[:, i : i + 1], shp[g][:, u, :], ALU.mult, ALU.mult
                )
                add_up(acc_p[h], prof[g][:, u, :], i)

        def light(g, parts):
            h = 2 * g // DEAL
            if h not in acc_w:
                acc_w[h] = open_sums("accw%d" % h, 2 * h + 1)
            if g not in lits:
                lits[g] = keep.tile([P, 2, N], F32, name="lit%d" % g)
            lit = lits[g]
            for part in parts:
                nc.vector.tensor_tensor(lit[:, part, :], prof[g][:, part, :], irr[g][:, part, :], ALU.mult)
                for u in range(part.start, part.stop):
                    add_up(acc_w[h], lit[:, u, :], 2 * g + u)

        whole = [slice(0, 2)]
        profile(0, add_exponentials(0, [slice(0, 1), slice(1, 2)]))
        both = add_exponentials(1, whole)
        light(0, whole)
        profile(1, both)
        both = add_exponentials(2, whole)
        light(1, whole)
        sum_pairs(den[0], acc_p[0])
        profile(2, both)
        both = add_exponentials(3, whole)
        light(2, whole)
        profile(3, both)
        sum_pairs(num[0], acc_w[0])
        light(3, [slice(0, 1)])
        sum_pairs(den[1], acc_p[1])
        light(3, [slice(1, 2)])
        sum_pairs(num[1], acc_w[1])

        res = keep.tile([P, M_BLOCKS, HALVES, POINTS], F32, name="res")
        for h in range(HALVES):
            root = keep.tile([P, M_BLOCKS, POINTS], F32, name="root%d" % h, tag="near%d" % (3 - h))
            inv = keep.tile([P, M_BLOCKS, POINTS], F32, name="inv%d" % h)
            nc.scalar.activation(root[:], den[h][:], ACT.Abs_reciprocal_sqrt, bias=0.1)
            nc.scalar.activation(inv[:], root[:], ACT.Square)
            nc.vector.tensor_tensor(res[:, :, h, :], num[h][:], inv[:], ALU.mult)
        nc.sync.dma_start(out.rearrange("(m p) v -> p m v", p=P), res[:].rearrange("p m h v -> p m (h v)"))
